import numpy as np
import ml_dtypes


def mxq(x, axis, fmt="e4m3"):
    dtype, down = {"e4m3": (ml_dtypes.float8_e4m3fn, 7), "e5m2": (ml_dtypes.float8_e5m2, 14)}[fmt]
    v = np.moveaxis(np.asarray(x, np.float32).astype(ml_dtypes.bfloat16).astype(np.float64), axis, -1)
    blocks = v.reshape(v.shape[:-1] + (-1, 32))
    amax = np.abs(blocks).max(-1, keepdims=True)
    byte = np.maximum(np.where(amax > 0, np.frexp(amax)[1] - 1 + 127, 0) - down, 1)
    scale = np.exp2(byte - 127.0)
    codes = (blocks / scale).astype(np.float32).astype(dtype).astype(np.float64)
    return np.moveaxis((codes * scale).reshape(v.shape), -1, axis)


WIDE = False


def mx_kscale(k):
    if not WIDE:
        return np.ones(k)
    levels = np.array([10, -10, 5, -5, 0])
    if k % 512:
        return np.exp2(np.random.permutation(np.resize(levels, k // 32))).repeat(32)
    a = np.empty((k // 512, 16))
    for p in range(k // 512):
        a[p, :8] = np.random.permutation(np.resize(levels, 8))
        for g in range(8):
            far = levels[np.abs(levels - a[p, g]) >= 10]
            a[p, g + 8] = far[np.random.randint(len(far))]
    return np.exp2(a.ravel()).repeat(32)


def f64(x):
    return np.asarray(x).astype(np.float64)


def striped(idx):
    return np.tile(np.asarray(idx).reshape(-1, 16).T, (8, 1)).astype(np.uint16)


def unstriped(offs):
    return offs[:16].T.reshape(-1).astype(np.int64)


E2M1 = np.array([0.0, 0.5, 1.0, 1.5, 2.0, 3.0, 4.0, 6.0, -0.0, -0.5, -1.0, -1.5, -2.0, -3.0, -4.0, -6.0])


def pack_weight(w, fmt):
    k, n = w.shape
    w = f64(np.asarray(w, np.float32).astype(ml_dtypes.bfloat16)).reshape(k // 32, 32, n)
    amax = np.abs(w).max(1)
    if fmt == "e4m3":
        byte = np.frexp(amax)[1] - 1 + 127 - 7
    else:
        mant, ex = np.frexp(amax / 6.0)
        byte = np.where(mant > 0.5, ex, ex - 1) + 127
    byte = np.clip(np.where(amax > 0, byte, 1), 1, 254)
    scaled = (w * np.exp2(127.0 - byte)[:, None, :]).reshape(k, n).astype(np.float32)
    by_word = np.ascontiguousarray(scaled.reshape(k // 512, 128, 4, n).transpose(0, 1, 3, 2))
    if fmt == "e4m3":
        words = by_word.astype(ml_dtypes.float8_e4m3fn).view(np.uint8)
    else:
        c = by_word.astype(ml_dtypes.float4_e2m1fn).view(np.uint8) & 0xF
        words = (c[..., 0::2] | (c[..., 1::2] << 4)).reshape(k // 512, 128, 2 * n)
    return np.ascontiguousarray(words), np.ascontiguousarray(byte.astype(np.uint8).reshape(k // 512, 16, n))


def unpack_weight(words, scales, fmt):
    g, _, n = scales.shape
    words = np.ascontiguousarray(words).reshape(g, 128, n, -1)
    if fmt == "e4m3":
        vals = words.view(ml_dtypes.float8_e4m3fn).astype(np.float64)
    else:
        nib = np.empty((g, 128, n, 4), np.uint8)
        nib[..., 0::2] = words & 0xF
        nib[..., 1::2] = words >> 4
        vals = E2M1[nib]
    vals = vals * np.repeat(np.exp2(scales.astype(np.float64) - 127.0), 8, axis=1)[..., None]
    return vals.transpose(0, 1, 3, 2).reshape(g * 512, n)


def silu(v):
    return v / (1.0 + np.exp(-v))


def bf(x):
    return np.asarray(x, np.float32).astype(ml_dtypes.bfloat16)


def planes(Y):
    r, m = Y.shape
    b = f64(bf(Y)).reshape(r // 32, 32, m)
    amax = np.abs(b).max(1)
    byte = np.clip(np.where(amax > 0, np.frexp(amax)[1] - 1 + 127 - 7, 1), 1, 254)
    codes = (b * np.exp2(127.0 - byte)[:, None, :]).reshape(r, m).astype(np.float32).astype(ml_dtypes.float8_e4m3fn).view(np.uint8)
    words = codes.reshape(r // 512, 128, 4, m).transpose(0, 1, 3, 2)
    return np.ascontiguousarray(words), np.ascontiguousarray(byte.astype(np.uint8).reshape(r // 512, 16, m))


K, T, J, L, V, N = 1024, 2048, 512, 512, 512, 512


def setup_inputs():
    n = np.random.standard_normal
    idx = np.random.permutation(T)[:J]
    idx2 = np.random.randint(0, V, J)
    fk = mx_kscale(K)
    fl = mx_kscale(L)
    xqp = pack_weight(n((K, T)) / fk[:, None], "e2m1")
    typ = pack_weight(n((L, V)) / fl[:, None], "e2m1")
    wtp = pack_weight(n((L, N)) * 1 / np.sqrt(L) * fl[:, None], "e4m3")
    return {
        "xq_words": xqp[0],
        "xq_scales": xqp[1],
        "wa": (n((K, N)) * 1 / np.sqrt(K) * fk[:, None]).astype(np.float32),
        "ty_words": typ[0],
        "ty_scales": typ[1],
        "wt_words": wtp[0],
        "wt_scales": wtp[1],
        "offs": striped(idx),
        "offs2": striped(idx2),
    }


def reference(xq_words, xq_scales, wa, ty_words, ty_scales, wt_words, wt_scales, offs, offs2):
    idx = unstriped(offs)
    idx2 = unstriped(offs2)
    xqu = unpack_weight(xq_words, xq_scales, "e2m1")
    tyu = unpack_weight(ty_words, ty_scales, "e2m1")
    wtu = unpack_weight(wt_words, wt_scales, "e4m3")
    waq = mxq(f64(wa), 0, "e4m3")
    xqidxg = xqu[:, idx]
    p = waq.T @ xqidxg
    e = wtu.T @ tyu
    y = silu(p + e[:, idx2])
    words, scales = planes(y)
    return y, words, scales

@@ -1,0 +1,280 @@
+from contextlib import ExitStack
+
+import concourse.mybir as mybir
+
+K, T, J, L, V, N = 1024, 2048, 512, 512, 512, 512
+FLOPS = 2 * K * N * J + 2 * L * N * V
+
+F32 = mybir.dt.float32
+BF16 = mybir.dt.bfloat16
+I32 = mybir.dt.int32
+U32 = mybir.dt.uint32
+U16 = mybir.dt.uint16
+U8 = mybir.dt.uint8
+FP8X4 = mybir.dt.float8_e4m3fn_x4
+FP4X4 = mybir.dt.float4_e2m1fn_x4
+ADD = mybir.AluOpType.add
+SILU = mybir.ActivationFunctionType.Silu
+
+P = 128
+PACK = 4
+PASSES = K // (P * PACK)
+QUADS = 4
+QUAD = P // QUADS
+ROWS = 4
+CHUNK = 128
+CHUNKS = J // CHUNK
+HALF = J // 2
+LIST_COLS = J // 16
+
+
+def tile_list_expert_typed_slots_pl_kernel(
+    tc, xq_words, xq_scales, wa, ty_words, ty_scales, wt_words, wt_scales, offs, offs2, out_0, out_1, out_2
+):
+    nc = tc.nc
+    with ExitStack() as ctx:
+        keep = ctx.enter_context(tc.tile_pool(name="keep", bufs=1))
+        psum = ctx.enter_context(tc.psum_pool(name="psum", bufs=1))
+
+        def sb(name, shape, dtype, tag=None):
+            return keep.tile(shape, dtype, name=name, tag=tag or name, align_bytes=64)
+
+        offs_sb = keep.tile([P, LIST_COLS], U16, name="offs_sb")
+        offs2_sb = keep.tile([P, LIST_COLS], U16, name="offs2_sb")
+        xq_sb = [sb("xq_sb%d" % a, [P, T], U16) for a in range(PASSES)]
+        xs_sb = sb("xs_sb", [P, T], U8)
+        xq_g = [sb("xq_g%d" % a, [P, J], U16) for a in range(PASSES)]
+        xs_g = [sb("xs_g%d" % a, [P, J], U8) for a in range(PASSES)]
+        ty_sb = sb("ty_sb", [P, V], U16)
+        tys_sb = sb("tys_sb", [P, V], U8)
+        wt_sb = sb("wt_sb", [P, N], I32)
+        wts_sb = sb("wts_sb", [P, N], U8)
+        wt_d = sb("wt_d", [P, N], I32)
+        wts_d = sb("wts_d", [P, N], U8)
+        wa_raw = [[sb("wa_raw%d%d" % (a, h), [P, PACK, N // 2], F32) for h in range(2)] for a in range(PASSES)]
+        wa_bf = [sb("wa_bf%d" % a, [P, PACK * N], BF16) for a in range(PASSES)]
+        wa_q = {}
+        wa_s = [sb("wa_s%d" % a, [P, N], U8) for a in range(PASSES)]
+        e_sb = {}
+        e_g = {}
+        z_sb = [sb("z_sb%d" % c, [P, PACK, CHUNK], F32) for c in range(CHUNKS)]
+        y_sb = [sb("y_sb%d" % c, [P, PACK, CHUNK], F32) for c in range(CHUNKS)]
+        y_bf = [sb("y_bf%d" % c, [P, CHUNK * PACK], BF16) for c in range(CHUNKS)]
+        y_q = sb("y_q", [P, J], U32)
+        y_s = sb("y_s", [P, J], U8)
+        e_ps = [psum.tile([P, V], F32, name="e_ps%d" % t) for t in range(PACK)]
+        p_ps = [psum.tile([P, PACK, CHUNK], F32, name="p_ps%d" % c) for c in range(CHUNKS)]
+
+        nc.vector.memset(wts_sb[:].bitcast(I32), 0)
+        nc.vector.memset(xs_sb[QUAD : 2 * QUAD, :].bitcast(I32), 0)
+        nc.vector.memset(xs_sb[2 * QUAD : P, :].bitcast(I32), 0)
+        for plane in (tys_sb, xs_g[0], xs_g[1]):
+            nc.vector.memset(plane[:].bitcast(I32), 0)
+        xs_rows = sb("xs_rows", [P, J], U8)
+
+        def gather_xs():
+            nc.vector.tensor_copy(xs_rows[:], xs_sb[:].indirect(offs_sb[:]))
+
+        def spread_xs(a):
+            for q in range(QUADS):
+                first = (a * QUADS + q) * ROWS
+                nc.sync.dma_start(
+                    out=xs_g[a][q * QUAD : q * QUAD + ROWS, :].bitcast(I32),
+                    in_=xs_rows[first : first + ROWS, :].bitcast(I32),
+                )
+
+        def load_wa(a, h):
+            rows = wa[a * P * PACK : (a + 1) * P * PACK, h * (N // 2) : (h + 1) * (N // 2)]
+            nc.sync.dma_start(out=wa_raw[a][h][:], in_=rows.rearrange("(p i) n -> p i n", i=PACK))
+
+        def load_plane(plane, scales):
+            for q in range(QUADS):
+                nc.sync.dma_start(
+                    out=plane[q * QUAD : q * QUAD + ROWS, :].bitcast(I32),
+                    in_=scales[0, q * ROWS : (q + 1) * ROWS, :].bitcast(I32),
+                )
+
+        def load_xs():
+            nc.sync.dma_start(out=xs_sb[0:QUAD, :].bitcast(I32), in_=xq_scales.rearrange("a q t -> (a q) t").bitcast(I32))
+
+        def load_xq(a):
+            nc.sync.dma_start(out=xq_sb[a][:].bitcast(I32), in_=xq_words[a].bitcast(I32))
+
+        nc.sync.dma_start(offs_sb[:], offs)
+        load_xs()
+        nc.sync.dma_start(out=wt_sb[:], in_=wt_words[0].rearrange("p n r -> p (n r)").bitcast(I32))
+        load_plane(wts_sb, wt_scales)
+        load_xq(0)
+        load_xq(1)
+        nc.sync.dma_start(out=ty_sb[:].bitcast(I32), in_=ty_words[0].bitcast(I32))
+        load_plane(tys_sb, ty_scales)
+        nc.sync.dma_start(offs2_sb[:], offs2)
+        load_wa(0, 0)
+        load_wa(0, 1)
+        gather_xs()
+        spread_xs(0)
+        load_wa(1, 0)
+        load_wa(1, 1)
+        spread_xs(1)
+
+        def cast_wa(a, h, copy):
+            dst = wa_bf[a][:].rearrange("p (t m i) -> p m i t", t=PACK, i=PACK)[:, h * (P // 2) : (h + 1) * (P // 2)]
+            copy(dst, wa_raw[a][h][:].rearrange("p i (m t) -> p m i t", t=PACK))
+
+        def quantise_wa(a, tag=None):
+            wa_q[a] = sb("wa_q%d" % a, [P, N], U32, tag)
+            nc.vector.quantize_mx(out=wa_q[a][:].bitcast(FP8X4), scales=wa_s[a][:], in_=wa_bf[a][:])
+
+        def multiply_p(a, chunks):
+            for c in chunks:
+                cols = slice(c * CHUNK, (c + 1) * CHUNK)
+                for t in range(PACK):
+                    rows = slice(t * P, (t + 1) * P)
+                    nc.tensor.matmul_mx(
+                        out=p_ps[c][:, t, :],
+                        lhsT=wa_q[a][:, rows].bitcast(FP8X4),
+                        lhsT_scale=wa_s[a][:, rows],
+                        rhs=xq_g[a][:, cols].bitcast(FP4X4),
+                        rhs_scale=xs_g[a][:, cols],
+                        start=(a == 0 and t == 0),
+                        stop=(a == PASSES - 1 and t == PACK - 1),
+                    )
+
+        def open_g(first, count, tag):
+            tile = sb("e_g%d" % first, [P, PACK, count * CHUNK], F32, tag)
+            for r in range(count):
+                e_g[first + r] = (tile, first, count)
+
+        def gather_e(c, count, t):
+            tile, first, held = e_g[c]
+            picks = offs2_sb[:, c * CHUNK // 16 : (c + count) * CHUNK // 16]
+            cols = slice((c - first) * CHUNK, (c - first + count) * CHUNK)
+            nc.vector.tensor_copy(tile[:, t, cols], e_sb[t].indirect(picks))
+
+        def add(c):
+            tile, first, count = e_g[c]
+            r = c - first
+            nc.vector.tensor_tensor(z_sb[c][:], p_ps[c][:], tile[:, :, r * CHUNK : (r + 1) * CHUNK], ADD)
+
+        out_rows = out_0.rearrange("(p t) j -> p t j", t=PACK)
+        out_words = out_1[0].rearrange("p j r -> p (j r)").bitcast(I32)
+
+        def activate(c):
+            nc.scalar.activation(y_sb[c][:], z_sb[c][:], SILU)
+            nc.sync.dma_start(out=out_rows[:, :, c * CHUNK : (c + 1) * CHUNK], in_=y_sb[c][:])
+
+        def cast_y(c, copy):
+            copy(
+                y_bf[c][:].rearrange("p (b j t) -> p b t j", j=4, t=PACK),
+                y_sb[c][:].rearrange("p t (b j) -> p b t j", j=4),
+            )
+
+        def quantise_y(c):
+            cols = slice(c * CHUNK, (c + 1) * CHUNK)
+            nc.vector.quantize_mx(out=y_q[:, cols].bitcast(FP8X4), scales=y_s[:, cols], in_=y_bf[c][:])
+
+        def store_words(h):
+            cols = slice(h * HALF, (h + 1) * HALF)
+            nc.sync.dma_start(out=out_words[:, cols], in_=y_q[:, cols].bitcast(I32))
+
+        def deal_words():
+            nc.vector.tensor_copy(
+                wt_d[:].rearrange("p (t a b) -> p a t b", t=PACK, b=4),
+                wt_sb[:].rearrange("p (a b t) -> p a t b", t=PACK, b=4),
+            )
+
+        def deal_scales():
+            nc.vector.tensor_copy(
+                wts_d[:].rearrange("p (t m) -> p t m", t=PACK),
+                wts_sb[:].rearrange("p (m t) -> p t m", t=PACK),
+            )
+
+        def multiply_e(t):
+            rows = slice(t * P, (t + 1) * P)
+            nc.tensor.matmul_mx(
+                out=e_ps[t][:],
+                lhsT=wt_d[:, rows].bitcast(FP8X4),
+                lhsT_scale=wts_d[:, rows],
+                rhs=ty_sb[:].bitcast(FP4X4),
+                rhs_scale=tys_sb[:],
+                start=True,
+                stop=True,
+            )
+
+        def open_e(first, tag=None):
+            pair = sb("e_sb%d" % first, [P, 2 * V], F32, tag)
+            e_sb[first] = pair[:, 0:V]
+            e_sb[first + 1] = pair[:, V : 2 * V]
+
+        def copy_e(t):
+            nc.scalar.copy(e_sb[t], e_ps[t][:])
+
+        def gather_xq(a):
+            nc.vector.tensor_copy(xq_g[a][:], xq_sb[a][:].indirect(offs_sb[:]))
+
+        def store_scales():
+            for q in range(QUADS):
+                queue = nc.scalar if q % 2 == 0 else nc.sync
+                queue.dma_start(
+                    out=out_2[0, q * ROWS : (q + 1) * ROWS, :].bitcast(I32),
+                    in_=y_s[q * QUAD : q * QUAD + ROWS, :].bitcast(I32),
+                )
+
+        on_v = nc.vector.tensor_copy
+        on_s = nc.scalar.copy
+        deal_words()
+        deal_scales()
+        gather_xq(0)
+        gather_xq(1)
+        multiply_e(0)
+        multiply_e(1)
+        multiply_e(2)
+        multiply_e(3)
+        open_e(0)
+        copy_e(0)
+        copy_e(1)
+        cast_wa(0, 0, on_s)
+        open_e(2, "wa_raw00")
+        copy_e(2)
+        copy_e(3)
+        cast_wa(1, 0, on_s)
+        open_g(0, 2, "e_g0")
+        gather_e(0, 2, 0)
+        gather_e(0, 2, 1)
+        cast_wa(0, 1, on_v)
+        quantise_wa(0)
+        multiply_p(0, range(CHUNKS))
+        gather_e(0, 2, 2)
+        gather_e(0, 2, 3)
+        cast_wa(1, 1, on_v)
+        quantise_wa(1)
+        multiply_p(1, range(CHUNKS))
+        open_g(2, 1, "wa_bf1")
+        gather_e(2, 1, 0)
+        gather_e(2, 1, 1)
+        gather_e(2, 1, 2)
+        gather_e(2, 1, 3)
+        add(0)
+        activate(0)
+        cast_y(0, on_s)
+        add(1)
+        activate(1)
+        cast_y(1, on_s)
+        add(2)
+        activate(2)
+        cast_y(2, on_s)
+        open_g(3, 1, "e_g0")
+        gather_e(3, 1, 0)
+        gather_e(3, 1, 1)
+        gather_e(3, 1, 2)
+        gather_e(3, 1, 3)
+        add(3)
+        activate(3)
+        quantise_y(0)
+        quantise_y(1)
+        store_words(0)
+        quantise_y(2)
+        cast_y(3, on_v)
+        quantise_y(3)
+        store_words(1)
+        store_scales()

@@ -105,10 +105,10 @@ def tile_list_expert_typed_slots_pl_kernel(
         nc.sync.dma_start(out=wt_sb[:], in_=wt_words[0].rearrange("p n r -> p (n r)").bitcast(I32))
         load_plane(wts_sb, wt_scales)
         load_xq(0)
-        load_xq(1)
         nc.sync.dma_start(out=ty_sb[:].bitcast(I32), in_=ty_words[0].bitcast(I32))
         load_plane(tys_sb, ty_scales)
         nc.sync.dma_start(offs2_sb[:], offs2)
+        load_xq(1)
         load_wa(0, 0)
         load_wa(0, 1)
         gather_xs()
@@ -119,13 +119,15 @@ def tile_list_expert_typed_slots_pl_kernel(
 
         def cast_wa(a, h, copy):
             dst = wa_bf[a][:].rearrange("p (t m i) -> p m i t", t=PACK, i=PACK)[:, h * (P // 2) : (h + 1) * (P // 2)]
-            copy(dst, wa_raw[a][h][:].rearrange("p i (m t) -> p m i t", t=PACK))
+            src = wa_raw[a][h][:].rearrange("p i (m t) -> p m i t", t=PACK)
+            for t in range(0, PACK, 2):
+                copy(dst[:, :, :, t : t + 2], src[:, :, :, t : t + 2])
 
         def quantise_wa(a, tag=None):
             wa_q[a] = sb("wa_q%d" % a, [P, N], U32, tag)
             nc.vector.quantize_mx(out=wa_q[a][:].bitcast(FP8X4), scales=wa_s[a][:], in_=wa_bf[a][:])
 
-        def multiply_p(a, chunks):
+        def multiply_p(a, chunks, opens):
             for c in chunks:
                 cols = slice(c * CHUNK, (c + 1) * CHUNK)
                 for t in range(PACK):
@@ -136,8 +138,8 @@ def tile_list_expert_typed_slots_pl_kernel(
                         lhsT_scale=wa_s[a][:, rows],
                         rhs=xq_g[a][:, cols].bitcast(FP4X4),
                         rhs_scale=xs_g[a][:, cols],
-                        start=(a == 0 and t == 0),
-                        stop=(a == PASSES - 1 and t == PACK - 1),
+                        start=(opens and t == 0),
+                        stop=(not opens and t == PACK - 1),
                     )
 
         def open_g(first, count, tag):
@@ -225,56 +227,55 @@ def tile_list_expert_typed_slots_pl_kernel(
         deal_words()
         deal_scales()
         gather_xq(0)
-        gather_xq(1)
         multiply_e(0)
         multiply_e(1)
         multiply_e(2)
         multiply_e(3)
         open_e(0)
+        open_e(2)
         copy_e(0)
         copy_e(1)
-        cast_wa(0, 0, on_s)
-        open_e(2, "wa_raw00")
         copy_e(2)
         copy_e(3)
+        cast_wa(0, 0, on_s)
+        cast_wa(0, 1, on_s)
         cast_wa(1, 0, on_s)
-        open_g(0, 2, "e_g0")
-        gather_e(0, 2, 0)
-        gather_e(0, 2, 1)
-        cast_wa(0, 1, on_v)
+        open_g(0, 3, "e_g0")
+        gather_e(0, 3, 0)
+        gather_xq(1)
+        gather_e(0, 3, 1)
+        gather_e(0, 3, 2)
+        gather_e(0, 3, 3)
         quantise_wa(0)
-        multiply_p(0, range(CHUNKS))
-        gather_e(0, 2, 2)
-        gather_e(0, 2, 3)
+        multiply_p(0, [0, 1], True)
         cast_wa(1, 1, on_v)
         quantise_wa(1)
-        multiply_p(1, range(CHUNKS))
-        open_g(2, 1, "wa_bf1")
-        gather_e(2, 1, 0)
-        gather_e(2, 1, 1)
-        gather_e(2, 1, 2)
-        gather_e(2, 1, 3)
-        add(0)
-        activate(0)
-        cast_y(0, on_s)
-        add(1)
-        activate(1)
-        cast_y(1, on_s)
-        add(2)
-        activate(2)
-        cast_y(2, on_s)
-        open_g(3, 1, "e_g0")
+        multiply_p(1, [0, 1], False)
+        multiply_p(1, [2], True)
+        multiply_p(0, [2], False)
+        multiply_p(1, [3], True)
+        multiply_p(0, [3], False)
+        open_g(3, 1, "wa_bf1")
         gather_e(3, 1, 0)
         gather_e(3, 1, 1)
         gather_e(3, 1, 2)
         gather_e(3, 1, 3)
+        add(0)
+        activate(0)
+        add(1)
+        activate(1)
+        add(2)
+        activate(2)
         add(3)
         activate(3)
+        cast_y(0, on_v)
+        cast_y(1, on_v)
         quantise_y(0)
         quantise_y(1)
         store_words(0)
-        quantise_y(2)
+        cast_y(2, on_s)
         cast_y(3, on_v)
         quantise_y(3)
+        quantise_y(2)
         store_words(1)
         store_scales()

@@ -51,7 +51,7 @@ def tile_list_expert_typed_slots_pl_kernel(
         wts_sb = sb("wts_sb", [P, N], U8)
         wt_d = sb("wt_d", [P, N], I32)
         wts_d = sb("wts_d", [P, N], U8)
-        wa_raw = [[sb("wa_raw%d%d" % (a, h), [P, PACK, N // 2], F32) for h in range(2)] for a in range(PASSES)]
+        wa_raw = [sb("wa_raw%d" % a, [P, PACK, N], F32) for a in range(PASSES)]
         wa_bf = [sb("wa_bf%d" % a, [P, PACK * N], BF16) for a in range(PASSES)]
         wa_q = {}
         wa_s = [sb("wa_s%d" % a, [P, N], U8) for a in range(PASSES)]
@@ -83,9 +83,9 @@ def tile_list_expert_typed_slots_pl_kernel(
                     in_=xs_rows[first : first + ROWS, :].bitcast(I32),
                 )
 
-        def load_wa(a, h):
-            rows = wa[a * P * PACK : (a + 1) * P * PACK, h * (N // 2) : (h + 1) * (N // 2)]
-            nc.sync.dma_start(out=wa_raw[a][h][:], in_=rows.rearrange("(p i) n -> p i n", i=PACK))
+        def load_wa(a):
+            rows = wa[a * P * PACK : (a + 1) * P * PACK, :]
+            nc.sync.dma_start(out=wa_raw[a][:], in_=rows.rearrange("(p i) n -> p i n", i=PACK))
 
         def load_plane(plane, scales):
             for q in range(QUADS):
@@ -109,19 +109,17 @@ def tile_list_expert_typed_slots_pl_kernel(
         load_plane(tys_sb, ty_scales)
         nc.sync.dma_start(offs2_sb[:], offs2)
         load_xq(1)
-        load_wa(0, 0)
-        load_wa(0, 1)
+        load_wa(0)
         gather_xs()
         spread_xs(0)
-        load_wa(1, 0)
-        load_wa(1, 1)
+        load_wa(1)
         spread_xs(1)
 
         def cast_wa(a, h, copy):
-            dst = wa_bf[a][:].rearrange("p (t m i) -> p m i t", t=PACK, i=PACK)[:, h * (P // 2) : (h + 1) * (P // 2)]
-            src = wa_raw[a][h][:].rearrange("p i (m t) -> p m i t", t=PACK)
-            for t in range(0, PACK, 2):
-                copy(dst[:, :, :, t : t + 2], src[:, :, :, t : t + 2])
+            dst = wa_bf[a][:].rearrange("p (t m i) -> p m i t", t=PACK, i=PACK)
+            src = wa_raw[a][:].rearrange("p i (m t) -> p m i t", t=PACK)
+            pair = slice(2 * h, 2 * h + 2)
+            copy(dst[:, :, :, pair], src[:, :, :, pair])
 
         def quantise_wa(a, tag=None):
             wa_q[a] = sb("wa_q%d" % a, [P, N], U32, tag)
@@ -247,12 +245,10 @@ def tile_list_expert_typed_slots_pl_kernel(
         gather_e(0, 3, 2)
         gather_e(0, 3, 3)
         quantise_wa(0)
-        multiply_p(0, [0, 1], True)
+        multiply_p(0, [0, 1, 2], True)
         cast_wa(1, 1, on_v)
         quantise_wa(1)
-        multiply_p(1, [0, 1], False)
-        multiply_p(1, [2], True)
-        multiply_p(0, [2], False)
+        multiply_p(1, [0, 1, 2], False)
         multiply_p(1, [3], True)
         multiply_p(0, [3], False)
         open_g(3, 1, "wa_bf1")

from contextlib import ExitStack

import concourse.mybir as mybir

K, T, J, L, V, N = 1024, 2048, 512, 512, 512, 512
FLOPS = 2 * K * N * J + 2 * L * N * V

F32 = mybir.dt.float32
BF16 = mybir.dt.bfloat16
I32 = mybir.dt.int32
U32 = mybir.dt.uint32
U16 = mybir.dt.uint16
U8 = mybir.dt.uint8
FP8X4 = mybir.dt.float8_e4m3fn_x4
FP4X4 = mybir.dt.float4_e2m1fn_x4
ADD = mybir.AluOpType.add
SILU = mybir.ActivationFunctionType.Silu

P = 128
PACK = 4
PASSES = K // (P * PACK)
QUADS = 4
QUAD = P // QUADS
ROWS = 4
CHUNK = 128
CHUNKS = J // CHUNK
HALF = J // 2
LIST_COLS = J // 16


def tile_list_expert_typed_slots_pl_kernel(
    tc, xq_words, xq_scales, wa, ty_words, ty_scales, wt_words, wt_scales, offs, offs2, out_0, out_1, out_2
):
    nc = tc.nc
    with ExitStack() as ctx:
        keep = ctx.enter_context(tc.tile_pool(name="keep", bufs=1))
        psum = ctx.enter_context(tc.psum_pool(name="psum", bufs=1))

        def sb(name, shape, dtype, tag=None):
            return keep.tile(shape, dtype, name=name, tag=tag or name, align_bytes=64)

        offs_sb = keep.tile([P, LIST_COLS], U16, name="offs_sb")
        offs2_sb = keep.tile([P, LIST_COLS], U16, name="offs2_sb")
        xq_sb = [sb("xq_sb%d" % a, [P, T], U16) for a in range(PASSES)]
        xs_sb = sb("xs_sb", [P, T], U8)
        xq_g = [sb("xq_g%d" % a, [P, J], U16) for a in range(PASSES)]
        xs_g = [sb("xs_g%d" % a, [P, J], U8) for a in range(PASSES)]
        ty_sb = sb("ty_sb", [P, V], U16)
        tys_sb = sb("tys_sb", [P, V], U8)
        wt_sb = sb("wt_sb", [P, N], I32)
        wts_sb = sb("wts_sb", [P, N], U8)
        wt_d = sb("wt_d", [P, N], I32)
        wts_d = sb("wts_d", [P, N], U8)
        wa_raw = [sb("wa_raw%d" % a, [P, PACK, N], F32) for a in range(PASSES)]
        wa_bf = [sb("wa_bf%d" % a, [P, PACK * N], BF16) for a in range(PASSES)]
        wa_q = {}
        wa_s = [sb("wa_s%d" % a, [P, N], U8) for a in range(PASSES)]
        e_sb = {}
        e_g = {}
        z_sb = [sb("z_sb%d" % c, [P, PACK, CHUNK], F32) for c in range(CHUNKS)]
        y_sb = [sb("y_sb%d" % c, [P, PACK, CHUNK], F32) for c in range(CHUNKS)]
        y_bf = [sb("y_bf%d" % c, [P, CHUNK * PACK], BF16) for c in range(CHUNKS)]
        y_q = sb("y_q", [P, J], U32)
        y_s = sb("y_s", [P, J], U8)
        e_ps = [psum.tile([P, V], F32, name="e_ps%d" % t) for t in range(PACK)]
        p_ps = [psum.tile([P, PACK, CHUNK], F32, name="p_ps%d" % c) for c in range(CHUNKS)]

        nc.vector.memset(wts_sb[:].bitcast(I32), 0)
        nc.vector.memset(xs_sb[QUAD : 2 * QUAD, :].bitcast(I32), 0)
        nc.vector.memset(xs_sb[2 * QUAD : P, :].bitcast(I32), 0)
        for plane in (tys_sb, xs_g[0], xs_g[1]):
            nc.vector.memset(plane[:].bitcast(I32), 0)
        xs_rows = sb("xs_rows", [P, J], U8)

        def gather_xs():
            nc.vector.tensor_copy(xs_rows[:], xs_sb[:].indirect(offs_sb[:]))

        def spread_xs(a):
            for q in range(QUADS):
                first = (a * QUADS + q) * ROWS
                nc.sync.dma_start(
                    out=xs_g[a][q * QUAD : q * QUAD + ROWS, :].bitcast(I32),
                    in_=xs_rows[first : first + ROWS, :].bitcast(I32),
                )

        def load_wa(a):
            rows = wa[a * P * PACK : (a + 1) * P * PACK, :]
            nc.sync.dma_start(out=wa_raw[a][:], in_=rows.rearrange("(p i) n -> p i n", i=PACK))

        def load_plane(plane, scales):
            for q in range(QUADS):
                nc.sync.dma_start(
                    out=plane[q * QUAD : q * QUAD + ROWS, :].bitcast(I32),
                    in_=scales[0, q * ROWS : (q + 1) * ROWS, :].bitcast(I32),
                )

        def load_xs():
            nc.sync.dma_start(out=xs_sb[0:QUAD, :].bitcast(I32), in_=xq_scales.rearrange("a q t -> (a q) t").bitcast(I32))

        def load_xq(a):
            nc.sync.dma_start(out=xq_sb[a][:].bitcast(I32), in_=xq_words[a].bitcast(I32))

        nc.sync.dma_start(offs_sb[:], offs)
        load_xs()
        nc.sync.dma_start(out=wt_sb[:], in_=wt_words[0].rearrange("p n r -> p (n r)").bitcast(I32))
        load_plane(wts_sb, wt_scales)
        load_xq(0)
        nc.sync.dma_start(out=ty_sb[:].bitcast(I32), in_=ty_words[0].bitcast(I32))
        load_plane(tys_sb, ty_scales)
        nc.sync.dma_start(offs2_sb[:], offs2)
        load_xq(1)
        load_wa(0)
        gather_xs()
        spread_xs(0)
        load_wa(1)
        spread_xs(1)

        def cast_wa(a, h, copy):
            dst = wa_bf[a][:].rearrange("p (t m i) -> p m i t", t=PACK, i=PACK)
            src = wa_raw[a][:].rearrange("p i (m t) -> p m i t", t=PACK)
            pair = slice(2 * h, 2 * h + 2)
            copy(dst[:, :, :, pair], src[:, :, :, pair])

        def quantise_wa(a, tag=None):
            wa_q[a] = sb("wa_q%d" % a, [P, N], U32, tag)
            nc.vector.quantize_mx(out=wa_q[a][:].bitcast(FP8X4), scales=wa_s[a][:], in_=wa_bf[a][:])

        def multiply_p(a, chunks, opens):
            for c in chunks:
                cols = slice(c * CHUNK, (c + 1) * CHUNK)
                for t in range(PACK):
                    rows = slice(t * P, (t + 1) * P)
                    nc.tensor.matmul_mx(
                        out=p_ps[c][:, t, :],
                        lhsT=wa_q[a][:, rows].bitcast(FP8X4),
                        lhsT_scale=wa_s[a][:, rows],
                        rhs=xq_g[a][:, cols].bitcast(FP4X4),
                        rhs_scale=xs_g[a][:, cols],
                        start=(opens and t == 0),
                        stop=(not opens and t == PACK - 1),
                    )

        def open_g(first, count, tag):
            tile = sb("e_g%d" % first, [P, PACK, count * CHUNK], F32, tag)
            for r in range(count):
                e_g[first + r] = (tile, first, count)

        def gather_e(c, count, t):
            tile, first, held = e_g[c]
            picks = offs2_sb[:, c * CHUNK // 16 : (c + count) * CHUNK // 16]
            cols = slice((c - first) * CHUNK, (c - first + count) * CHUNK)
            nc.vector.tensor_copy(tile[:, t, cols], e_sb[t].indirect(picks))

        def add(c):
            tile, first, count = e_g[c]
            r = c - first
            nc.vector.tensor_tensor(z_sb[c][:], p_ps[c][:], tile[:, :, r * CHUNK : (r + 1) * CHUNK], ADD)

        out_rows = out_0.rearrange("(p t) j -> p t j", t=PACK)
        out_words = out_1[0].rearrange("p j r -> p (j r)").bitcast(I32)

        def activate(c):
            nc.scalar.activation(y_sb[c][:], z_sb[c][:], SILU)
            nc.sync.dma_start(out=out_rows[:, :, c * CHUNK : (c + 1) * CHUNK], in_=y_sb[c][:])

        def cast_y(c, copy):
            copy(
                y_bf[c][:].rearrange("p (b j t) -> p b t j", j=4, t=PACK),
                y_sb[c][:].rearrange("p t (b j) -> p b t j", j=4),
            )

        def quantise_y(c):
            cols = slice(c * CHUNK, (c + 1) * CHUNK)
            nc.vector.quantize_mx(out=y_q[:, cols].bitcast(FP8X4), scales=y_s[:, cols], in_=y_bf[c][:])

        def store_words(h):
            cols = slice(h * HALF, (h + 1) * HALF)
            nc.sync.dma_start(out=out_words[:, cols], in_=y_q[:, cols].bitcast(I32))

        def deal_words():
            nc.vector.tensor_copy(
                wt_d[:].rearrange("p (t a b) -> p a t b", t=PACK, b=4),
                wt_sb[:].rearrange("p (a b t) -> p a t b", t=PACK, b=4),
            )

        def deal_scales():
            nc.vector.tensor_copy(
                wts_d[:].rearrange("p (t m) -> p t m", t=PACK),
                wts_sb[:].rearrange("p (m t) -> p t m", t=PACK),
            )

        def multiply_e(t):
            rows = slice(t * P, (t + 1) * P)
            nc.tensor.matmul_mx(
                out=e_ps[t][:],
                lhsT=wt_d[:, rows].bitcast(FP8X4),
                lhsT_scale=wts_d[:, rows],
                rhs=ty_sb[:].bitcast(FP4X4),
                rhs_scale=tys_sb[:],
                start=True,
                stop=True,
            )

        def open_e(first, tag=None):
            pair = sb("e_sb%d" % first, [P, 2 * V], F32, tag)
            e_sb[first] = pair[:, 0:V]
            e_sb[first + 1] = pair[:, V : 2 * V]

        def copy_e(t):
            nc.scalar.copy(e_sb[t], e_ps[t][:])

        def gather_xq(a):
            nc.vector.tensor_copy(xq_g[a][:], xq_sb[a][:].indirect(offs_sb[:]))

        def store_scales():
            for q in range(QUADS):
                queue = nc.scalar if q % 2 == 0 else nc.sync
                queue.dma_start(
                    out=out_2[0, q * ROWS : (q + 1) * ROWS, :].bitcast(I32),
                    in_=y_s[q * QUAD : q * QUAD + ROWS, :].bitcast(I32),
                )

        on_v = nc.vector.tensor_copy
        on_s = nc.scalar.copy
        deal_words()
        deal_scales()
        gather_xq(0)
        multiply_e(0)
        multiply_e(1)
        multiply_e(2)
        multiply_e(3)
        open_e(0)
        open_e(2)
        copy_e(0)
        copy_e(1)
        copy_e(2)
        copy_e(3)
        cast_wa(0, 0, on_s)
        cast_wa(0, 1, on_s)
        cast_wa(1, 0, on_s)
        open_g(0, 3, "e_g0")
        gather_e(0, 3, 0)
        gather_xq(1)
        gather_e(0, 3, 1)
        gather_e(0, 3, 2)
        gather_e(0, 3, 3)
        quantise_wa(0)
        multiply_p(0, [0, 1, 2], True)
        cast_wa(1, 1, on_v)
        quantise_wa(1)
        multiply_p(1, [0, 1, 2], False)
        multiply_p(1, [3], True)
        multiply_p(0, [3], False)
        open_g(3, 1, "wa_bf1")
        gather_e(3, 1, 0)
        gather_e(3, 1, 1)
        gather_e(3, 1, 2)
        gather_e(3, 1, 3)
        add(0)
        activate(0)
        add(1)
        activate(1)
        add(2)
        activate(2)
        add(3)
        activate(3)
        cast_y(0, on_v)
        cast_y(1, on_v)
        quantise_y(0)
        quantise_y(1)
        store_words(0)
        cast_y(2, on_s)
        cast_y(3, on_v)
        quantise_y(3)
        quantise_y(2)
        store_words(1)
        store_scales()
